import numpy as np
import ml_dtypes


def mxq(x, axis, fmt="e4m3"):
    dtype, down = {"e4m3": (ml_dtypes.float8_e4m3fn, 7), "e5m2": (ml_dtypes.float8_e5m2, 14)}[fmt]
    v = np.moveaxis(np.asarray(x, np.float32).astype(ml_dtypes.bfloat16).astype(np.float64), axis, -1)
    blocks = v.reshape(v.shape[:-1] + (-1, 32))
    amax = np.abs(blocks).max(-1, keepdims=True)
    byte = np.maximum(np.where(amax > 0, np.frexp(amax)[1] - 1 + 127, 0) - down, 1)
    scale = np.exp2(byte - 127.0)
    codes = (blocks / scale).astype(np.float32).astype(dtype).astype(np.float64)
    return np.moveaxis((codes * scale).reshape(v.shape), -1, axis)


WIDE = False


def mx_kscale(k):
    if not WIDE:
        return np.ones(k)
    levels = np.array([10, -10, 5, -5, 0])
    if k % 512:
        return np.exp2(np.random.permutation(np.resize(levels, k // 32))).repeat(32)
    a = np.empty((k // 512, 16))
    for p in range(k // 512):
        a[p, :8] = np.random.permutation(np.resize(levels, 8))
        for g in range(8):
            far = levels[np.abs(levels - a[p, g]) >= 10]
            a[p, g + 8] = far[np.random.randint(len(far))]
    return np.exp2(a.ravel()).repeat(32)


def f64(x):
    return np.asarray(x).astype(np.float64)


def striped(idx):
    return np.tile(np.asarray(idx).reshape(-1, 16).T, (8, 1)).astype(np.uint16)


def unstriped(offs):
    return offs[:16].T.reshape(-1).astype(np.int64)


def striped8(idx):
    return np.asarray(idx).reshape(8, -1, 16).transpose(0, 2, 1).reshape(128, -1).astype(np.uint16)


def unstriped8(offs):
    return offs.reshape(8, 16, -1).transpose(0, 2, 1).reshape(8, -1).astype(np.int64)


def pick8(x, idx, run):
    r = np.arange(len(x))
    return x[r[:, None], idx[r % (8 * run) // run]]


E2M1 = np.array([0.0, 0.5, 1.0, 1.5, 2.0, 3.0, 4.0, 6.0, -0.0, -0.5, -1.0, -1.5, -2.0, -3.0, -4.0, -6.0])


def pack_weight(w, fmt):
    k, n = w.shape
    w = f64(np.asarray(w, np.float32).astype(ml_dtypes.bfloat16)).reshape(k // 32, 32, n)
    amax = np.abs(w).max(1)
    if fmt == "e4m3":
        byte = np.frexp(amax)[1] - 1 + 127 - 7
    else:
        mant, ex = np.frexp(amax / 6.0)
        byte = np.where(mant > 0.5, ex, ex - 1) + 127
    byte = np.clip(np.where(amax > 0, byte, 1), 1, 254)
    scaled = (w * np.exp2(127.0 - byte)[:, None, :]).reshape(k, n).astype(np.float32)
    by_word = np.ascontiguousarray(scaled.reshape(k // 512, 128, 4, n).transpose(0, 1, 3, 2))
    if fmt == "e4m3":
        words = by_word.astype(ml_dtypes.float8_e4m3fn).view(np.uint8)
    else:
        c = by_word.astype(ml_dtypes.float4_e2m1fn).view(np.uint8) & 0xF
        words = (c[..., 0::2] | (c[..., 1::2] << 4)).reshape(k // 512, 128, 2 * n)
    return np.ascontiguousarray(words), np.ascontiguousarray(byte.astype(np.uint8).reshape(k // 512, 16, n))


def unpack_weight(words, scales, fmt):
    g, _, n = scales.shape
    words = np.ascontiguousarray(words).reshape(g, 128, n, -1)
    if fmt == "e4m3":
        vals = words.view(ml_dtypes.float8_e4m3fn).astype(np.float64)
    else:
        nib = np.empty((g, 128, n, 4), np.uint8)
        nib[..., 0::2] = words & 0xF
        nib[..., 1::2] = words >> 4
        vals = E2M1[nib]
    vals = vals * np.repeat(np.exp2(scales.astype(np.float64) - 127.0), 8, axis=1)[..., None]
    return vals.transpose(0, 1, 3, 2).reshape(g * 512, n)


K, J, R, T, C, N, S, U = 512, 384, 512, 2048, 512, 256, 1024, 1024


def setup_inputs():
    n = np.random.standard_normal
    idx = np.random.permutation(T)[:J]
    idx2 = np.stack([np.random.permutation(C)[:J] for _ in range(8)])
    idx3 = np.stack([np.random.permutation(C)[:J] for _ in range(8)])
    idx4 = np.random.permutation(S)[:N]
    idx5 = np.stack([np.random.permutation(U)[:C] for _ in range(8)])
    idx6 = np.stack([np.random.permutation(U)[:C] for _ in range(8)])
    fk = mx_kscale(K)
    fr = mx_kscale(R)
    xtp = pack_weight(n((K, T)) * fk[:, None], "e4m3")
    wp = pack_weight(n((K, R)) * 1 / np.sqrt(K) / fk[:, None] * fr, "e2m1")
    w2p = pack_weight(n((K, R)) * 1 / np.sqrt(K) / fk[:, None] * fr, "e4m3")
    vsp = pack_weight(n((R, S)) * 1 / np.sqrt(R) / fr[:, None], "e4m3")
    return {
        "xt_words": xtp[0],
        "xt_scales": xtp[1],
        "w_words": wp[0],
        "w_scales": wp[1],
        "w2_words": w2p[0],
        "w2_scales": w2p[1],
        "vs_words": vsp[0],
        "vs_scales": vsp[1],
        "offs": striped(idx),
        "offs2": striped8(idx2),
        "offs3": striped8(idx3),
        "offs4": striped(idx4),
        "offs5": striped8(idx5),
        "offs6": striped8(idx6),
    }


def reference(xt_words, xt_scales, w_words, w_scales, w2_words, w2_scales, vs_words, vs_scales, offs, offs2, offs3, offs4, offs5, offs6):
    idx = unstriped(offs)
    idx2 = unstriped8(offs2)
    idx3 = unstriped8(offs3)
    idx4 = unstriped(offs4)
    idx5 = unstriped8(offs5)
    idx6 = unstriped8(offs6)
    xtu = unpack_weight(xt_words, xt_scales, "e4m3")
    wu = unpack_weight(w_words, w_scales, "e2m1")
    w2u = unpack_weight(w2_words, w2_scales, "e4m3")
    vsu = unpack_weight(vs_words, vs_scales, "e4m3")
    xtidxg = xtu[:, idx]
    a = wu.T @ xtidxg
    b = w2u.T @ xtidxg
    pw = np.zeros((R, C))
    pw[np.arange(R)[:, None], idx2[np.arange(R) % 512 // 64]] = a
    pv = np.zeros((R, C))
    pv[np.arange(R)[:, None], idx3[np.arange(R) % 512 // 64]] = b
    hid = np.minimum(np.abs(pw), np.abs(pv))
    vsidx4g = vsu[:, idx4]
    hidq = mxq(hid, 0, "e4m3")
    p = vsidx4g.T @ hidq
    m0 = np.zeros((N, U))
    m0[np.arange(N)[:, None], idx5[np.arange(N) % 128 // 16]] = p
    m1 = np.zeros((N, U))
    m1[np.arange(N)[:, None], idx6[np.arange(N) % 128 // 16]] = p
    y = m0 - m1
    return y

@@ -1,0 +1,209 @@
+from contextlib import ExitStack
+
+import concourse.mybir as mybir
+
+K, J, R, T, C, N, S, U = 512, 384, 512, 2048, 512, 256, 1024, 1024
+FLOPS = 2 * (2 * K * R * J + R * N * C)
+
+F32 = mybir.dt.float32
+BF16 = mybir.dt.bfloat16
+I32 = mybir.dt.int32
+U32 = mybir.dt.uint32
+U16 = mybir.dt.uint16
+U8 = mybir.dt.uint8
+FP8X4 = mybir.dt.float8_e4m3fn_x4
+FP4X4 = mybir.dt.float4_e2m1fn_x4
+ACT = mybir.ActivationFunctionType
+ALU = mybir.AluOpType
+
+P = 128
+PACK = 4
+QUAD = 32
+LIST_ROWS = 16
+FIRST = 128
+BOARD_CHUNKS = ((0, 64), (64, 128), (128, 256), (256, 512))
+PAGE_PIECES = ((0, 0, 64), (1, 0, 64), (0, 64, 256), (0, 256, 512), (1, 64, 512))
+STORE_COLS = 256
+
+
+def tile_picked_tokens_plain_twin_bothlanded_store_divergence_kernel(
+    tc, xt_words, xt_scales, w_words, w_scales, w2_words, w2_scales, vs_words, vs_scales,
+    offs, offs2, offs3, offs4, offs5, offs6, out,
+):
+    nc = tc.nc
+
+    with ExitStack() as ctx:
+        lists = ctx.enter_context(tc.tile_pool(name="lists", bufs=1))
+        sb = ctx.enter_context(tc.tile_pool(name="sb", bufs=1))
+        ring = ctx.enter_context(tc.tile_pool(name="ring", bufs=2))
+        psum = ctx.enter_context(tc.psum_pool(name="psum", bufs=8))
+
+        def load_list(dram, name):
+            tile = lists.tile(list(dram.shape), U16, name=name)
+            nc.sync.dma_start(tile[:], dram)
+            return tile
+
+        def entries(list_tile, lo, hi):
+            return list_tile[:, lo // LIST_ROWS : hi // LIST_ROWS]
+
+        def words_view(dram):
+            return dram[0].rearrange("p c b -> p (c b)").bitcast(I32)
+
+        def zeroed(engine, shape, dtype, name, tag):
+            tile = sb.tile(shape, dtype, name=name, tag=tag, align_bytes=64)
+            engine.memset(tile[:].bitcast(I32), 0)
+            return tile
+
+        def load_weight_scales(dram, name):
+            rows = sb.tile([PACK, PACK, R // 4], I32, name=name, tag="weight_scale_rows", align_bytes=64)
+            nc.scalar.dma_start(rows[:], dram[0].bitcast(I32).rearrange("(q i) c -> i q c", i=PACK))
+            return rows
+
+        def deal_weight_scales(rows, name):
+            plane = zeroed(nc.vector, [P, R], U8, name + "_plane", name + "_plane")
+            for q in range(PACK):
+                nc.vector.tensor_copy(plane[QUAD * q : QUAD * q + PACK, :].bitcast(I32), rows[:, q, :])
+            dealt = sb.tile([P, R], U8, name=name + "_dealt", align_bytes=64)
+            nc.vector.tensor_copy(
+                dealt[:].rearrange("p (t m) -> p t m", t=PACK), plane[:].rearrange("p (m t) -> p t m", t=PACK)
+            )
+            return dealt
+
+        tok_list = load_list(offs, "tok_list")
+        w_scale_rows = load_weight_scales(w_scales, "w_scale_rows")
+        xs_rows = sb.tile([P, 2, T // 4], I32, name="xs_rows", tag="xs_rows", align_bytes=64)
+        for half, queue in enumerate((nc.sync, nc.scalar)):
+            queue.dma_start(
+                xs_rows[64 * half : 64 * half + PACK, :, :],
+                xt_scales[0, 8 * half : 8 * half + 8, :].bitcast(I32).rearrange("(q i) c -> i q c", i=PACK),
+            )
+        w_raw = sb.tile([P, 2 * R], U8, name="w_raw", tag="weight_raw", align_bytes=64)
+        nc.sync.dma_start(w_raw[:].bitcast(I32), w_words[0].bitcast(I32))
+        xw_win = sb.tile([P, T], I32, name="xw_win", tag="word_window", align_bytes=64)
+        nc.sync.dma_start(xw_win[:], words_view(xt_words))
+        pw_list = load_list(offs2, "pw_list")
+        pv_list = load_list(offs3, "pv_list")
+        vs_list = load_list(offs4, "vs_list")
+        page_lists = [load_list(offs5, "m0_list"), load_list(offs6, "m1_list")]
+
+        xs_win = zeroed(nc.vector, [P, T], U8, "xs_win", "scale_window")
+        w_sc = deal_weight_scales(w_scale_rows, "w_sc")
+        w_dealt = sb.tile([P, 2 * R], U8, name="w_dealt", align_bytes=64)
+        nc.scalar.copy(
+            w_dealt[:].bitcast(U16).rearrange("p (t m) -> p t m", t=PACK),
+            w_raw[:].bitcast(U16).rearrange("p (m t) -> p t m", t=PACK),
+        )
+        for q in range(PACK):
+            src = 64 * (q // 2)
+            nc.vector.tensor_copy(
+                xs_win[QUAD * q : QUAD * q + PACK, :].bitcast(I32), xs_rows[src : src + PACK, q % 2, :]
+            )
+        xg_sc = sb.tile([P, J], U8, name="xg_sc", align_bytes=64)
+        nc.vector.tensor_copy(xg_sc[:], xs_win[:].indirect(tok_list[:]))
+        xg = sb.tile([P, J], U32, name="xg", align_bytes=64)
+        for lo, hi in ((0, FIRST), (FIRST, J)):
+            nc.vector.tensor_copy(xg[:, lo:hi], xw_win[:].bitcast(U32).indirect(entries(tok_list, lo, hi)))
+
+        pw = [zeroed(nc.vector, [P, C], F32, "pw%d" % t, "pw%d" % t) for t in range(PACK)]
+
+        def slot_product(weights, weight_scales, lo, hi):
+            acc = psum.tile([P, hi - lo], F32, name="acc", tag="bank")
+            for a, b in ((0, FIRST), (FIRST, J)):
+                if lo <= a and b <= hi:
+                    nc.tensor.matmul_mx(
+                        out=acc[:, a - lo : b - lo], lhsT=weights, lhsT_scale=weight_scales,
+                        rhs=xg[:, a:b].bitcast(FP8X4), rhs_scale=xg_sc[:, a:b], start=True, stop=True,
+                    )
+            return acc
+
+        def magnitude(dst, acc):
+            plain = ring.tile([P, J], F32, name="plain")
+            width = acc.shape[1]
+            nc.vector.tensor_copy(plain[:, :width], acc[:])
+            nc.vector.scalar_tensor_tensor(dst, acc[:], -1.0, plain[:, :width], ALU.mult, ALU.max)
+
+        def scatter(window, list_tile, values, lo, hi):
+            nc.scalar.activation(window[:].indirect(entries(list_tile, lo, hi)), values[:, lo:hi], ACT.Copy)
+
+        a_abs = [sb.tile([P, J], F32, name="a_abs%d" % t, tag="slot%d" % t, align_bytes=64) for t in range(PACK)]
+        a_pieces = [(0, 0, FIRST), (1, 0, FIRST), (0, FIRST, J), (1, FIRST, J), (2, 0, J), (3, 0, J)]
+        for i, (t, lo, hi) in enumerate(a_pieces):
+            acc = slot_product(
+                w_dealt[:, 2 * P * t : 2 * P * (t + 1)].bitcast(FP4X4), w_sc[:, P * t : P * (t + 1)], lo, hi
+            )
+            if i == 0:
+                nc.scalar.activation(a_abs[t][:, lo:hi], acc[:], ACT.Abs)
+            else:
+                magnitude(a_abs[t][:, lo:hi], acc)
+            scatter(pw[t], pw_list, a_abs[t], lo, hi)
+
+        w2_scale_rows = load_weight_scales(w2_scales, "w2_scale_rows")
+        w2_raw = sb.tile([P, R], I32, name="w2_raw", tag="weight_raw", align_bytes=64)
+        nc.sync.dma_start(w2_raw[:], words_view(w2_words))
+        vw_win = sb.tile([P, S], I32, name="vw_win", tag="word_window", align_bytes=64)
+        nc.sync.dma_start(vw_win[:], words_view(vs_words))
+        vs_win = zeroed(nc.vector, [P, S], U8, "vs_win", "scale_window")
+        for q in range(PACK):
+            nc.sync.dma_start(
+                vs_win[QUAD * q : QUAD * q + PACK, :].bitcast(I32),
+                vs_scales[0, PACK * q : PACK * (q + 1), :].bitcast(I32),
+            )
+        w2_sc = deal_weight_scales(w2_scale_rows, "w2_sc")
+        w2_dealt = sb.tile([P, R], I32, name="w2_dealt", align_bytes=64)
+        nc.vector.tensor_copy(
+            w2_dealt[:].rearrange("p (t m) -> p t m", t=PACK), w2_raw[:].rearrange("p (m t) -> p t m", t=PACK)
+        )
+        pv = []
+        for t in range(PACK):
+            acc = slot_product(w2_dealt[:, P * t : P * (t + 1)].bitcast(FP8X4), w2_sc[:, P * t : P * (t + 1)], 0, J)
+            b_abs = sb.tile([P, J], F32, name="b_abs%d" % t, align_bytes=64)
+            magnitude(b_abs[:], acc)
+            pv.append(zeroed(nc.gpsimd, [P, C], F32, "pv%d" % t, "slot%d" % t))
+            scatter(pv[t], pv_list, b_abs, 0, J)
+
+        vg_sc = sb.tile([P, N], U8, name="vg_sc", align_bytes=64)
+        nc.vector.tensor_copy(vg_sc[:], vs_win[:].indirect(vs_list[:]))
+        vg = sb.tile([P, N], U32, name="vg", align_bytes=64)
+        nc.vector.tensor_copy(vg[:], vw_win[:].bitcast(U32).indirect(vs_list[:]))
+
+        page_tags = (("xs_rows", "weight_raw"), ("word_window", "scale_window"))
+        pages = [
+            [zeroed(nc.gpsimd, [P, U], F32, "m%d_%d" % (side, g), page_tags[g][side]) for side in range(2)]
+            for g in range(N // P)
+        ]
+
+        hid = [sb.tile([P, hi - lo, PACK], BF16, name="hid%d" % lo, align_bytes=64) for lo, hi in BOARD_CHUNKS]
+
+        def meet(t, i):
+            lo, hi = BOARD_CHUNKS[i]
+            nc.vector.tensor_tensor(hid[i][:, :, t], pw[t][:, lo:hi], pv[t][:, lo:hi], ALU.min)
+
+        for t in range(PACK - 1):
+            for i in range(len(BOARD_CHUNKS)):
+                meet(t, i)
+        p_sb = [sb.tile([P, C], F32, name="p_sb%d" % g, align_bytes=64) for g in range(N // P)]
+        for i, (lo, hi) in enumerate(BOARD_CHUNKS):
+            meet(PACK - 1, i)
+            codes = sb.tile([P, hi - lo], U32, name="codes%d" % lo, align_bytes=64)
+            scales = sb.tile([P, hi - lo], U8, name="scales%d" % lo, align_bytes=64)
+            nc.vector.quantize_mx(codes[:].bitcast(FP8X4), scales[:], hid[i][:].rearrange("p c t -> p (c t)"))
+            for g in range(N // P):
+                acc = psum.tile([P, hi - lo], F32, name="acc", tag="bank")
+                nc.tensor.matmul_mx(
+                    out=acc[:], lhsT=vg[:, P * g : P * (g + 1)].bitcast(FP8X4), lhsT_scale=vg_sc[:, P * g : P * (g + 1)],
+                    rhs=codes[:].bitcast(FP8X4), rhs_scale=scales[:], start=True, stop=True,
+                )
+                if i == 0:
+                    nc.scalar.copy(p_sb[g][:, lo:hi], acc[:])
+                else:
+                    nc.vector.tensor_copy(p_sb[g][:, lo:hi], acc[:])
+
+        for g, lo, hi in PAGE_PIECES:
+            for side in range(2):
+                scatter(pages[g][side], page_lists[side], p_sb[g], lo, hi)
+        for g in range(N // P):
+            for i, u0 in enumerate(range(0, U, STORE_COLS)):
+                cols = slice(u0, u0 + STORE_COLS)
+                diff = sb.tile([P, STORE_COLS], F32, name="diff%d_%d" % (g, i), align_bytes=64)
+                nc.vector.tensor_tensor(diff[:], pages[g][0][:, cols], pages[g][1][:, cols], ALU.subtract)
+                nc.sync.dma_start(out[P * g : P * (g + 1), cols], diff[:])

@@ -23,7 +23,7 @@ LIST_ROWS = 16
 FIRST = 128
 BOARD_CHUNKS = ((0, 64), (64, 128), (128, 256), (256, 512))
 PAGE_PIECES = ((0, 0, 64), (1, 0, 64), (0, 64, 256), (0, 256, 512), (1, 64, 512))
-STORE_COLS = 256
+STORE_PIECES = ((0, 256), (256, 512), (512, 768), (768, 1024))
 
 
 def tile_picked_tokens_plain_twin_bothlanded_store_divergence_kernel(
@@ -35,6 +35,7 @@ def tile_picked_tokens_plain_twin_bothlanded_store_divergence_kernel(
     with ExitStack() as ctx:
         lists = ctx.enter_context(tc.tile_pool(name="lists", bufs=1))
         sb = ctx.enter_context(tc.tile_pool(name="sb", bufs=1))
+        reuse = ctx.enter_context(tc.tile_pool(name="reuse", bufs=1))
         ring = ctx.enter_context(tc.tile_pool(name="ring", bufs=2))
         psum = ctx.enter_context(tc.psum_pool(name="psum", bufs=8))
 
@@ -49,46 +50,55 @@ def tile_picked_tokens_plain_twin_bothlanded_store_divergence_kernel(
         def words_view(dram):
             return dram[0].rearrange("p c b -> p (c b)").bitcast(I32)
 
-        def zeroed(engine, shape, dtype, name, tag):
-            tile = sb.tile(shape, dtype, name=name, tag=tag, align_bytes=64)
+        def zeroed(engine, tile):
             engine.memset(tile[:].bitcast(I32), 0)
             return tile
 
-        def load_weight_scales(dram, name):
-            rows = sb.tile([PACK, PACK, R // 4], I32, name=name, tag="weight_scale_rows", align_bytes=64)
-            nc.scalar.dma_start(rows[:], dram[0].bitcast(I32).rearrange("(q i) c -> i q c", i=PACK))
-            return rows
+        def after(tag, shape, dtype, name):
+            return sb.tile(shape, dtype, name=name, tag=tag, align_bytes=64)
 
-        def deal_weight_scales(rows, name):
-            plane = zeroed(nc.vector, [P, R], U8, name + "_plane", name + "_plane")
+        def placed(offset, shape, dtype, name):
+            return reuse.tile(shape, dtype, name=name, offset=offset, align_bytes=64)
+
+        def load_scale_plane(plane, dram):
             for q in range(PACK):
-                nc.vector.tensor_copy(plane[QUAD * q : QUAD * q + PACK, :].bitcast(I32), rows[:, q, :])
-            dealt = sb.tile([P, R], U8, name=name + "_dealt", align_bytes=64)
+                nc.sync.dma_start(
+                    plane[QUAD * q : QUAD * q + PACK, :].bitcast(I32),
+                    dram[0, PACK * q : PACK * (q + 1), :].bitcast(I32),
+                )
+
+        def deal_bytes(plane, dealt, t0, t1):
             nc.vector.tensor_copy(
-                dealt[:].rearrange("p (t m) -> p t m", t=PACK), plane[:].rearrange("p (m t) -> p t m", t=PACK)
+                dealt[:].rearrange("p (t m) -> p t m", m=P),
+                plane[:].rearrange("p (m t) -> p t m", t=PACK)[:, t0:t1, :],
             )
-            return dealt
 
         tok_list = load_list(offs, "tok_list")
-        w_scale_rows = load_weight_scales(w_scales, "w_scale_rows")
-        xs_rows = sb.tile([P, 2, T // 4], I32, name="xs_rows", tag="xs_rows", align_bytes=64)
+        ws_rows = sb.tile([PACK, PACK, R // 4], I32, name="ws_rows", align_bytes=64)
+        nc.scalar.dma_start(ws_rows[:], w_scales[0].bitcast(I32).rearrange("(q i) c -> i q c", i=PACK))
+        xs_rows = sb.tile([P, 2, T // 4], I32, name="xs_rows", align_bytes=64)
         for half, queue in enumerate((nc.sync, nc.scalar)):
             queue.dma_start(
                 xs_rows[64 * half : 64 * half + PACK, :, :],
                 xt_scales[0, 8 * half : 8 * half + 8, :].bitcast(I32).rearrange("(q i) c -> i q c", i=PACK),
             )
-        w_raw = sb.tile([P, 2 * R], U8, name="w_raw", tag="weight_raw", align_bytes=64)
+        w_raw = sb.tile([P, 2 * R], U8, name="w_raw", align_bytes=64)
         nc.sync.dma_start(w_raw[:].bitcast(I32), w_words[0].bitcast(I32))
-        xw_win = sb.tile([P, T], I32, name="xw_win", tag="word_window", align_bytes=64)
+        xw_win = placed(0, [P, T], I32, "xw_win")
         nc.sync.dma_start(xw_win[:], words_view(xt_words))
         pw_list = load_list(offs2, "pw_list")
         pv_list = load_list(offs3, "pv_list")
         vs_list = load_list(offs4, "vs_list")
         page_lists = [load_list(offs5, "m0_list"), load_list(offs6, "m1_list")]
 
-        xs_win = zeroed(nc.vector, [P, T], U8, "xs_win", "scale_window")
-        w_sc = deal_weight_scales(w_scale_rows, "w_sc")
-        w_dealt = sb.tile([P, 2 * R], U8, name="w_dealt", align_bytes=64)
+        w_plane = zeroed(nc.vector, sb.tile([P, R], U8, name="w_plane", align_bytes=64))
+        xs_win = zeroed(nc.vector, sb.tile([P, T], U8, name="xs_win", align_bytes=64))
+        pw = [zeroed(nc.vector, sb.tile([P, C], F32, name="pw%d" % t, align_bytes=64)) for t in range(2)]
+        for q in range(PACK):
+            nc.vector.tensor_copy(w_plane[QUAD * q : QUAD * q + PACK, :].bitcast(I32), ws_rows[:, q, :])
+        w_sc = [after("w_sc", [P, 2 * P], U8, "w_sc01")]
+        deal_bytes(w_plane, w_sc[0], 0, 2)
+        w_dealt = sb.tile([P, 2 * R], U8, name="w_dealt", tag="w_dealt", align_bytes=64)
         nc.scalar.copy(
             w_dealt[:].bitcast(U16).rearrange("p (t m) -> p t m", t=PACK),
             w_raw[:].bitcast(U16).rearrange("p (m t) -> p t m", t=PACK),
@@ -98,21 +108,23 @@ def tile_picked_tokens_plain_twin_bothlanded_store_divergence_kernel(
             nc.vector.tensor_copy(
                 xs_win[QUAD * q : QUAD * q + PACK, :].bitcast(I32), xs_rows[src : src + PACK, q % 2, :]
             )
-        xg_sc = sb.tile([P, J], U8, name="xg_sc", align_bytes=64)
-        nc.vector.tensor_copy(xg_sc[:], xs_win[:].indirect(tok_list[:]))
-        xg = sb.tile([P, J], U32, name="xg", align_bytes=64)
+        xg_sc_first = sb.tile([P, J - FIRST], U8, name="xg_sc_first", align_bytes=64)
+        nc.vector.tensor_copy(xg_sc_first[:], xs_win[:].indirect(entries(tok_list, 0, J - FIRST)))
+        xg = after("xg", [P, J], U32, "xg")
         for lo, hi in ((0, FIRST), (FIRST, J)):
             nc.vector.tensor_copy(xg[:, lo:hi], xw_win[:].bitcast(U32).indirect(entries(tok_list, lo, hi)))
-
-        pw = [zeroed(nc.vector, [P, C], F32, "pw%d" % t, "pw%d" % t) for t in range(PACK)]
+        xg_sc_rest = placed(7936, [P, J - FIRST], U8, "xg_sc_rest")
+        nc.vector.tensor_copy(xg_sc_rest[:], xs_win[:].indirect(entries(tok_list, FIRST, J)))
+        w_sc.append(placed(7680, [P, 2 * P], U8, "w_sc23"))
+        deal_bytes(w_plane, w_sc[1], 2, PACK)
 
         def slot_product(weights, weight_scales, lo, hi):
             acc = psum.tile([P, hi - lo], F32, name="acc", tag="bank")
-            for a, b in ((0, FIRST), (FIRST, J)):
+            for a, b, slot_scales in ((0, FIRST, xg_sc_first[:, :FIRST]), (FIRST, J, xg_sc_rest[:])):
                 if lo <= a and b <= hi:
                     nc.tensor.matmul_mx(
                         out=acc[:, a - lo : b - lo], lhsT=weights, lhsT_scale=weight_scales,
-                        rhs=xg[:, a:b].bitcast(FP8X4), rhs_scale=xg_sc[:, a:b], start=True, stop=True,
+                        rhs=xg[:, a:b].bitcast(FP8X4), rhs_scale=slot_scales, start=True, stop=True,
                     )
             return acc
 
@@ -125,40 +137,42 @@ def tile_picked_tokens_plain_twin_bothlanded_store_divergence_kernel(
         def scatter(window, list_tile, values, lo, hi):
             nc.scalar.activation(window[:].indirect(entries(list_tile, lo, hi)), values[:, lo:hi], ACT.Copy)
 
-        a_abs = [sb.tile([P, J], F32, name="a_abs%d" % t, tag="slot%d" % t, align_bytes=64) for t in range(PACK)]
+        a_sb = [sb.tile([P, J], F32, name="a_sb%d" % t, tag="slot%d" % t, align_bytes=64) for t in range(PACK)]
         a_pieces = [(0, 0, FIRST), (1, 0, FIRST), (0, FIRST, J), (1, FIRST, J), (2, 0, J), (3, 0, J)]
         for i, (t, lo, hi) in enumerate(a_pieces):
             acc = slot_product(
-                w_dealt[:, 2 * P * t : 2 * P * (t + 1)].bitcast(FP4X4), w_sc[:, P * t : P * (t + 1)], lo, hi
+                w_dealt[:, 2 * P * t : 2 * P * (t + 1)].bitcast(FP4X4), w_sc[t // 2][:, P * (t % 2) : P * (t % 2 + 1)], lo, hi
             )
             if i == 0:
-                nc.scalar.activation(a_abs[t][:, lo:hi], acc[:], ACT.Abs)
+                nc.scalar.activation(a_sb[t][:, lo:hi], acc[:], ACT.Copy)
             else:
-                magnitude(a_abs[t][:, lo:hi], acc)
-            scatter(pw[t], pw_list, a_abs[t], lo, hi)
+                nc.vector.tensor_copy(a_sb[t][:, lo:hi], acc[:])
+            if t < 2:
+                scatter(pw[t], pw_list, a_sb[t], lo, hi)
+        for t, tag in ((2, "w_dealt"), (3, "w_sc")):
+            pw.append(zeroed(nc.gpsimd, after(tag, [P, C], F32, "pw%d" % t)))
+            scatter(pw[t], pw_list, a_sb[t], 0, J)
 
-        w2_scale_rows = load_weight_scales(w2_scales, "w2_scale_rows")
-        w2_raw = sb.tile([P, R], I32, name="w2_raw", tag="weight_raw", align_bytes=64)
+        w2_raw = placed(4096, [P, R], I32, "w2_raw")
         nc.sync.dma_start(w2_raw[:], words_view(w2_words))
-        vw_win = sb.tile([P, S], I32, name="vw_win", tag="word_window", align_bytes=64)
+        w2_plane = zeroed(nc.gpsimd, placed(6144, [P, R], U8, "w2_plane"))
+        load_scale_plane(w2_plane, w2_scales)
+        vw_win = placed(0, [P, S], I32, "vw_win")
         nc.sync.dma_start(vw_win[:], words_view(vs_words))
-        vs_win = zeroed(nc.vector, [P, S], U8, "vs_win", "scale_window")
-        for q in range(PACK):
-            nc.sync.dma_start(
-                vs_win[QUAD * q : QUAD * q + PACK, :].bitcast(I32),
-                vs_scales[0, PACK * q : PACK * (q + 1), :].bitcast(I32),
-            )
-        w2_sc = deal_weight_scales(w2_scale_rows, "w2_sc")
-        w2_dealt = sb.tile([P, R], I32, name="w2_dealt", align_bytes=64)
+        vs_win = zeroed(nc.gpsimd, placed(6656, [P, S], U8, "vs_win"))
+        load_scale_plane(vs_win, vs_scales)
+        w2_sc = sb.tile([P, R], U8, name="w2_sc", align_bytes=64)
+        deal_bytes(w2_plane, w2_sc, 0, PACK)
+        w2_dealt = after("w2_dealt", [P, R], I32, "w2_dealt")
         nc.vector.tensor_copy(
             w2_dealt[:].rearrange("p (t m) -> p t m", t=PACK), w2_raw[:].rearrange("p (m t) -> p t m", t=PACK)
         )
         pv = []
         for t in range(PACK):
             acc = slot_product(w2_dealt[:, P * t : P * (t + 1)].bitcast(FP8X4), w2_sc[:, P * t : P * (t + 1)], 0, J)
-            b_abs = sb.tile([P, J], F32, name="b_abs%d" % t, align_bytes=64)
+            b_abs = after("b_abs%d" % t, [P, J], F32, "b_abs%d" % t)
             magnitude(b_abs[:], acc)
-            pv.append(zeroed(nc.gpsimd, [P, C], F32, "pv%d" % t, "slot%d" % t))
+            pv.append(zeroed(nc.gpsimd, after("slot%d" % t, [P, C], F32, "pv%d" % t)))
             scatter(pv[t], pv_list, b_abs, 0, J)
 
         vg_sc = sb.tile([P, N], U8, name="vg_sc", align_bytes=64)
@@ -166,17 +180,23 @@ def tile_picked_tokens_plain_twin_bothlanded_store_divergence_kernel(
         vg = sb.tile([P, N], U32, name="vg", align_bytes=64)
         nc.vector.tensor_copy(vg[:], vw_win[:].bitcast(U32).indirect(vs_list[:]))
 
-        page_tags = (("xs_rows", "weight_raw"), ("word_window", "scale_window"))
         pages = [
-            [zeroed(nc.gpsimd, [P, U], F32, "m%d_%d" % (side, g), page_tags[g][side]) for side in range(2)]
-            for g in range(N // P)
+            [placed(0, [P, U], F32, "m0_0"), placed(4096, [P, U], F32, "m1_0")],
+            [after("w2_dealt", [P, U], F32, "m0_1"), after("b_abs0", [P, U], F32, "m1_1")],
         ]
+        for g in range(N // P):
+            for side in range(2):
+                zeroed(nc.gpsimd, pages[g][side])
 
         hid = [sb.tile([P, hi - lo, PACK], BF16, name="hid%d" % lo, align_bytes=64) for lo, hi in BOARD_CHUNKS]
 
+        pw_abs = after("xg", [P, PACK, C], F32, "pw_abs")
+        for t in range(PACK):
+            nc.vector.scalar_tensor_tensor(pw_abs[:, t, :], pw[t][:], -1.0, pw[t][:], ALU.mult, ALU.max)
+
         def meet(t, i):
             lo, hi = BOARD_CHUNKS[i]
-            nc.vector.tensor_tensor(hid[i][:, :, t], pw[t][:, lo:hi], pv[t][:, lo:hi], ALU.min)
+            nc.vector.tensor_tensor(hid[i][:, :, t], pw_abs[:, t, lo:hi], pv[t][:, lo:hi], ALU.min)
 
         for t in range(PACK - 1):
             for i in range(len(BOARD_CHUNKS)):
@@ -202,8 +222,8 @@ def tile_picked_tokens_plain_twin_bothlanded_store_divergence_kernel(
             for side in range(2):
                 scatter(pages[g][side], page_lists[side], p_sb[g], lo, hi)
         for g in range(N // P):
-            for i, u0 in enumerate(range(0, U, STORE_COLS)):
-                cols = slice(u0, u0 + STORE_COLS)
-                diff = sb.tile([P, STORE_COLS], F32, name="diff%d_%d" % (g, i), align_bytes=64)
+            for lo, hi in STORE_PIECES:
+                cols = slice(lo, hi)
+                diff = sb.tile([P, hi - lo], F32, name="diff%d_%d" % (g, lo), align_bytes=64)
                 nc.vector.tensor_tensor(diff[:], pages[g][0][:, cols], pages[g][1][:, cols], ALU.subtract)
                 nc.sync.dma_start(out[P * g : P * (g + 1), cols], diff[:])

@@ -20,7 +20,8 @@ P = 128
 PACK = 4
 QUAD = 32
 LIST_ROWS = 16
-FIRST = 128
+SLOT_PIECE = 128
+SCALE_GATHER = 256
 BOARD_CHUNKS = ((0, 64), (64, 128), (128, 256), (256, 512))
 PAGE_PIECES = ((0, 0, 64), (1, 0, 64), (0, 64, 256), (0, 256, 512), (1, 64, 512))
 STORE_PIECES = ((0, 256), (256, 512), (512, 768), (768, 1024))
@@ -108,23 +109,28 @@ def tile_picked_tokens_plain_twin_bothlanded_store_divergence_kernel(
             nc.vector.tensor_copy(
                 xs_win[QUAD * q : QUAD * q + PACK, :].bitcast(I32), xs_rows[src : src + PACK, q % 2, :]
             )
-        xg_sc_first = sb.tile([P, J - FIRST], U8, name="xg_sc_first", align_bytes=64)
-        nc.vector.tensor_copy(xg_sc_first[:], xs_win[:].indirect(entries(tok_list, 0, J - FIRST)))
+        xg_sc_first = after("xg_sc_first", [P, SCALE_GATHER], U8, "xg_sc_first")
+        nc.vector.tensor_copy(xg_sc_first[:], xs_win[:].indirect(entries(tok_list, 0, SCALE_GATHER)))
         xg = after("xg", [P, J], U32, "xg")
-        for lo, hi in ((0, FIRST), (FIRST, J)):
+        for lo in range(0, J, SLOT_PIECE):
+            hi = lo + SLOT_PIECE
             nc.vector.tensor_copy(xg[:, lo:hi], xw_win[:].bitcast(U32).indirect(entries(tok_list, lo, hi)))
-        xg_sc_rest = placed(7936, [P, J - FIRST], U8, "xg_sc_rest")
-        nc.vector.tensor_copy(xg_sc_rest[:], xs_win[:].indirect(entries(tok_list, FIRST, J)))
-        w_sc.append(placed(7680, [P, 2 * P], U8, "w_sc23"))
+        xg_sc_rest = placed(7936, [P, SCALE_GATHER], U8, "xg_sc_rest")
+        nc.vector.tensor_copy(xg_sc_rest[:], xs_win[:].indirect(entries(tok_list, J - SCALE_GATHER, J)))
+        w_sc.append(placed(6144, [P, 2 * P], U8, "w_sc23"))
         deal_bytes(w_plane, w_sc[1], 2, PACK)
 
         def slot_product(weights, weight_scales, lo, hi):
             acc = psum.tile([P, hi - lo], F32, name="acc", tag="bank")
-            for a, b, slot_scales in ((0, FIRST, xg_sc_first[:, :FIRST]), (FIRST, J, xg_sc_rest[:])):
-                if lo <= a and b <= hi:
+            for base, slot_scales, a, b in (
+                (0, xg_sc_first, lo, min(hi, SCALE_GATHER)),
+                (J - SCALE_GATHER, xg_sc_rest, max(lo, SCALE_GATHER), hi),
+            ):
+                if a < b:
                     nc.tensor.matmul_mx(
                         out=acc[:, a - lo : b - lo], lhsT=weights, lhsT_scale=weight_scales,
-                        rhs=xg[:, a:b].bitcast(FP8X4), rhs_scale=slot_scales, start=True, stop=True,
+                        rhs=xg[:, a:b].bitcast(FP8X4), rhs_scale=slot_scales[:, a - base : b - base],
+                        start=True, stop=True,
                     )
             return acc
 
@@ -138,7 +144,7 @@ def tile_picked_tokens_plain_twin_bothlanded_store_divergence_kernel(
             nc.scalar.activation(window[:].indirect(entries(list_tile, lo, hi)), values[:, lo:hi], ACT.Copy)
 
         a_sb = [sb.tile([P, J], F32, name="a_sb%d" % t, tag="slot%d" % t, align_bytes=64) for t in range(PACK)]
-        a_pieces = [(0, 0, FIRST), (1, 0, FIRST), (0, FIRST, J), (1, FIRST, J), (2, 0, J), (3, 0, J)]
+        a_pieces = [(0, 0, 128), (1, 0, 256), (0, 128, J), (1, 256, J), (2, 0, J), (3, 0, J)]
         for i, (t, lo, hi) in enumerate(a_pieces):
             acc = slot_product(
                 w_dealt[:, 2 * P * t : 2 * P * (t + 1)].bitcast(FP4X4), w_sc[t // 2][:, P * (t % 2) : P * (t % 2 + 1)], lo, hi
@@ -159,7 +165,7 @@ def tile_picked_tokens_plain_twin_bothlanded_store_divergence_kernel(
         load_scale_plane(w2_plane, w2_scales)
         vw_win = placed(0, [P, S], I32, "vw_win")
         nc.sync.dma_start(vw_win[:], words_view(vs_words))
-        vs_win = zeroed(nc.gpsimd, placed(6656, [P, S], U8, "vs_win"))
+        vs_win = zeroed(nc.gpsimd, after("xg_sc_first", [P, S], U8, "vs_win"))
         load_scale_plane(vs_win, vs_scales)
         w2_sc = sb.tile([P, R], U8, name="w2_sc", align_bytes=64)
         deal_bytes(w2_plane, w2_sc, 0, PACK)

@@ -19,12 +19,26 @@ ALU = mybir.AluOpType
 P = 128
 PACK = 4
 QUAD = 32
+HALF = 64
 LIST_ROWS = 16
-SLOT_PIECE = 128
+ALIGN = 64
+
+WORD_GATHER = 128
 SCALE_GATHER = 256
-BOARD_CHUNKS = ((0, 64), (64, 128), (128, 256), (256, 512))
-PAGE_PIECES = ((0, 0, 64), (1, 0, 64), (0, 64, 256), (0, 256, 512), (1, 64, 512))
-STORE_PIECES = ((0, 256), (256, 512), (512, 768), (768, 1024))
+EARLY_BOARDS = 2
+FIRST_BOARD_PIECES = ((0, 0, 128), (1, 0, 256), (0, 128, J), (1, 256, J), (2, 0, J), (3, 0, J))
+BOARD_CHUNKS = ((0, 64), (64, 128), (128, 256), (256, 384), (384, 512))
+PAGE_PIECES = ((0, 0, 64), (1, 0, 64), (0, 64, 256), (0, 256, C), (1, 64, C))
+STORE_COLS = 256
+
+AT_TOKEN_WORDS = 0
+AT_STORE_WORDS = 0
+AT_W2_WORDS = 4096
+AT_W_SCALES_LATE = 6528
+AT_SLOT_SCALES_LATE = 7936
+AT_W2_SCALES = 6144
+AT_STORE_SCALES = 6656
+AT_PAGES = (0, 4096)
 
 
 def tile_picked_tokens_plain_twin_bothlanded_store_divergence_kernel(
@@ -55,148 +69,147 @@ def tile_picked_tokens_plain_twin_bothlanded_store_divergence_kernel(
             engine.memset(tile[:].bitcast(I32), 0)
             return tile
 
-        def after(tag, shape, dtype, name):
-            return sb.tile(shape, dtype, name=name, tag=tag, align_bytes=64)
+        def shared(tag, shape, dtype, name):
+            return sb.tile(shape, dtype, name=name, tag=tag, align_bytes=ALIGN)
 
         def placed(offset, shape, dtype, name):
-            return reuse.tile(shape, dtype, name=name, offset=offset, align_bytes=64)
+            return reuse.tile(shape, dtype, name=name, offset=offset, align_bytes=ALIGN)
 
-        def load_scale_plane(plane, dram):
+        def load_scale_rows(tile, dram):
             for q in range(PACK):
                 nc.sync.dma_start(
-                    plane[QUAD * q : QUAD * q + PACK, :].bitcast(I32),
+                    tile[QUAD * q : QUAD * q + PACK, :].bitcast(I32),
                     dram[0, PACK * q : PACK * (q + 1), :].bitcast(I32),
                 )
 
-        def deal_bytes(plane, dealt, t0, t1):
+        def deal_scales(scales, dealt, t0, t1):
             nc.vector.tensor_copy(
                 dealt[:].rearrange("p (t m) -> p t m", m=P),
-                plane[:].rearrange("p (m t) -> p t m", t=PACK)[:, t0:t1, :],
+                scales[:].rearrange("p (m t) -> p t m", t=PACK)[:, t0:t1, :],
             )
 
         tok_list = load_list(offs, "tok_list")
-        ws_rows = sb.tile([PACK, PACK, R // 4], I32, name="ws_rows", align_bytes=64)
+        ws_rows = sb.tile([PACK, PACK, R // 4], I32, name="ws_rows", align_bytes=ALIGN)
         nc.scalar.dma_start(ws_rows[:], w_scales[0].bitcast(I32).rearrange("(q i) c -> i q c", i=PACK))
-        xs_rows = sb.tile([P, 2, T // 4], I32, name="xs_rows", align_bytes=64)
+        xs_rows = sb.tile([P, 2, T // 4], I32, name="xs_rows", align_bytes=ALIGN)
         for half, queue in enumerate((nc.sync, nc.scalar)):
             queue.dma_start(
-                xs_rows[64 * half : 64 * half + PACK, :, :],
+                xs_rows[HALF * half : HALF * half + PACK, :, :],
                 xt_scales[0, 8 * half : 8 * half + 8, :].bitcast(I32).rearrange("(q i) c -> i q c", i=PACK),
             )
-        w_raw = sb.tile([P, 2 * R], U8, name="w_raw", align_bytes=64)
+        w_raw = sb.tile([P, 2 * R], U8, name="w_raw", align_bytes=ALIGN)
         nc.sync.dma_start(w_raw[:].bitcast(I32), w_words[0].bitcast(I32))
-        xw_win = placed(0, [P, T], I32, "xw_win")
+        xw_win = placed(AT_TOKEN_WORDS, [P, T], I32, "xw_win")
         nc.sync.dma_start(xw_win[:], words_view(xt_words))
         pw_list = load_list(offs2, "pw_list")
         pv_list = load_list(offs3, "pv_list")
         vs_list = load_list(offs4, "vs_list")
         page_lists = [load_list(offs5, "m0_list"), load_list(offs6, "m1_list")]
 
-        w_plane = zeroed(nc.vector, sb.tile([P, R], U8, name="w_plane", align_bytes=64))
-        xs_win = zeroed(nc.vector, sb.tile([P, T], U8, name="xs_win", align_bytes=64))
-        pw = [zeroed(nc.vector, sb.tile([P, C], F32, name="pw%d" % t, align_bytes=64)) for t in range(2)]
+        ws_spread = zeroed(nc.vector, sb.tile([P, R], U8, name="ws_spread", align_bytes=ALIGN))
+        xs_win = zeroed(nc.vector, sb.tile([P, T], U8, name="xs_win", align_bytes=ALIGN))
+        pw = [
+            zeroed(nc.vector, sb.tile([P, C], F32, name="pw%d" % t, align_bytes=ALIGN)) for t in range(EARLY_BOARDS)
+        ]
         for q in range(PACK):
-            nc.vector.tensor_copy(w_plane[QUAD * q : QUAD * q + PACK, :].bitcast(I32), ws_rows[:, q, :])
-        w_sc = [after("w_sc", [P, 2 * P], U8, "w_sc01")]
-        deal_bytes(w_plane, w_sc[0], 0, 2)
-        w_dealt = sb.tile([P, 2 * R], U8, name="w_dealt", tag="w_dealt", align_bytes=64)
+            nc.vector.tensor_copy(ws_spread[QUAD * q : QUAD * q + PACK, :].bitcast(I32), ws_rows[:, q, :])
+        ws_dealt = [shared("ws_early", [P, EARLY_BOARDS * P], U8, "ws_early")]
+        deal_scales(ws_spread, ws_dealt[0], 0, EARLY_BOARDS)
+        w_dealt = shared("w_dealt", [P, 2 * R], U8, "w_dealt")
         nc.scalar.copy(
             w_dealt[:].bitcast(U16).rearrange("p (t m) -> p t m", t=PACK),
             w_raw[:].bitcast(U16).rearrange("p (m t) -> p t m", t=PACK),
         )
         for q in range(PACK):
-            src = 64 * (q // 2)
+            row0 = HALF * (q // 2)
             nc.vector.tensor_copy(
-                xs_win[QUAD * q : QUAD * q + PACK, :].bitcast(I32), xs_rows[src : src + PACK, q % 2, :]
+                xs_win[QUAD * q : QUAD * q + PACK, :].bitcast(I32), xs_rows[row0 : row0 + PACK, q % 2, :]
             )
-        xg_sc_first = after("xg_sc_first", [P, SCALE_GATHER], U8, "xg_sc_first")
-        nc.vector.tensor_copy(xg_sc_first[:], xs_win[:].indirect(entries(tok_list, 0, SCALE_GATHER)))
-        xg = after("xg", [P, J], U32, "xg")
-        for lo in range(0, J, SLOT_PIECE):
-            hi = lo + SLOT_PIECE
+        xg_sc_early = sb.tile([P, SCALE_GATHER], U8, name="xg_sc_early", align_bytes=ALIGN)
+        nc.vector.tensor_copy(xg_sc_early[:], xs_win[:].indirect(entries(tok_list, 0, SCALE_GATHER)))
+        xg = shared("xg", [P, J], U32, "xg")
+        for lo in range(0, J, WORD_GATHER):
+            hi = lo + WORD_GATHER
             nc.vector.tensor_copy(xg[:, lo:hi], xw_win[:].bitcast(U32).indirect(entries(tok_list, lo, hi)))
-        xg_sc_rest = placed(7936, [P, SCALE_GATHER], U8, "xg_sc_rest")
-        nc.vector.tensor_copy(xg_sc_rest[:], xs_win[:].indirect(entries(tok_list, J - SCALE_GATHER, J)))
-        w_sc.append(placed(6144, [P, 2 * P], U8, "w_sc23"))
-        deal_bytes(w_plane, w_sc[1], 2, PACK)
+        xg_sc_late = placed(AT_SLOT_SCALES_LATE, [P, SCALE_GATHER], U8, "xg_sc_late")
+        nc.vector.tensor_copy(xg_sc_late[:], xs_win[:].indirect(entries(tok_list, J - SCALE_GATHER, J)))
+        ws_dealt.append(placed(AT_W_SCALES_LATE, [P, (PACK - EARLY_BOARDS) * P], U8, "ws_late"))
+        deal_scales(ws_spread, ws_dealt[1], EARLY_BOARDS, PACK)
 
         def slot_product(weights, weight_scales, lo, hi):
             acc = psum.tile([P, hi - lo], F32, name="acc", tag="bank")
-            for base, slot_scales, a, b in (
-                (0, xg_sc_first, lo, min(hi, SCALE_GATHER)),
-                (J - SCALE_GATHER, xg_sc_rest, max(lo, SCALE_GATHER), hi),
+            for base, slot_scales, c0, c1 in (
+                (0, xg_sc_early, lo, min(hi, SCALE_GATHER)),
+                (J - SCALE_GATHER, xg_sc_late, max(lo, SCALE_GATHER), hi),
             ):
-                if a < b:
+                if c0 < c1:
                     nc.tensor.matmul_mx(
-                        out=acc[:, a - lo : b - lo], lhsT=weights, lhsT_scale=weight_scales,
-                        rhs=xg[:, a:b].bitcast(FP8X4), rhs_scale=slot_scales[:, a - base : b - base],
+                        out=acc[:, c0 - lo : c1 - lo], lhsT=weights, lhsT_scale=weight_scales,
+                        rhs=xg[:, c0:c1].bitcast(FP8X4), rhs_scale=slot_scales[:, c0 - base : c1 - base],
                         start=True, stop=True,
                     )
             return acc
 
-        def magnitude(dst, acc):
-            plain = ring.tile([P, J], F32, name="plain")
-            width = acc.shape[1]
-            nc.vector.tensor_copy(plain[:, :width], acc[:])
-            nc.vector.scalar_tensor_tensor(dst, acc[:], -1.0, plain[:, :width], ALU.mult, ALU.max)
-
         def scatter(window, list_tile, values, lo, hi):
             nc.scalar.activation(window[:].indirect(entries(list_tile, lo, hi)), values[:, lo:hi], ACT.Copy)
 
-        a_sb = [sb.tile([P, J], F32, name="a_sb%d" % t, tag="slot%d" % t, align_bytes=64) for t in range(PACK)]
-        a_pieces = [(0, 0, 128), (1, 0, 256), (0, 128, J), (1, 256, J), (2, 0, J), (3, 0, J)]
-        for i, (t, lo, hi) in enumerate(a_pieces):
+        a_sb = [shared("a_then_pv%d" % t, [P, J], F32, "a_sb%d" % t) for t in range(PACK)]
+        for i, (t, lo, hi) in enumerate(FIRST_BOARD_PIECES):
+            part, place = divmod(t, EARLY_BOARDS)
             acc = slot_product(
-                w_dealt[:, 2 * P * t : 2 * P * (t + 1)].bitcast(FP4X4), w_sc[t // 2][:, P * (t % 2) : P * (t % 2 + 1)], lo, hi
+                w_dealt[:, 2 * P * t : 2 * P * (t + 1)].bitcast(FP4X4),
+                ws_dealt[part][:, P * place : P * (place + 1)], lo, hi,
             )
             if i == 0:
                 nc.scalar.activation(a_sb[t][:, lo:hi], acc[:], ACT.Copy)
             else:
                 nc.vector.tensor_copy(a_sb[t][:, lo:hi], acc[:])
-            if t < 2:
+            if t < EARLY_BOARDS:
                 scatter(pw[t], pw_list, a_sb[t], lo, hi)
-        for t, tag in ((2, "w_dealt"), (3, "w_sc")):
-            pw.append(zeroed(nc.gpsimd, after(tag, [P, C], F32, "pw%d" % t)))
+        for t, tag in zip(range(EARLY_BOARDS, PACK), ("w_dealt", "ws_early")):
+            pw.append(zeroed(nc.gpsimd, shared(tag, [P, C], F32, "pw%d" % t)))
             scatter(pw[t], pw_list, a_sb[t], 0, J)
 
-        w2_raw = placed(4096, [P, R], I32, "w2_raw")
+        w2_raw = placed(AT_W2_WORDS, [P, R], I32, "w2_raw")
         nc.sync.dma_start(w2_raw[:], words_view(w2_words))
-        w2_plane = zeroed(nc.gpsimd, placed(6144, [P, R], U8, "w2_plane"))
-        load_scale_plane(w2_plane, w2_scales)
-        vw_win = placed(0, [P, S], I32, "vw_win")
+        w2s_spread = zeroed(nc.gpsimd, placed(AT_W2_SCALES, [P, R], U8, "w2s_spread"))
+        load_scale_rows(w2s_spread, w2_scales)
+        vw_win = placed(AT_STORE_WORDS, [P, S], I32, "vw_win")
         nc.sync.dma_start(vw_win[:], words_view(vs_words))
-        vs_win = zeroed(nc.gpsimd, after("xg_sc_first", [P, S], U8, "vs_win"))
-        load_scale_plane(vs_win, vs_scales)
-        w2_sc = sb.tile([P, R], U8, name="w2_sc", align_bytes=64)
-        deal_bytes(w2_plane, w2_sc, 0, PACK)
-        w2_dealt = after("w2_dealt", [P, R], I32, "w2_dealt")
+        vs_win = zeroed(nc.gpsimd, placed(AT_STORE_SCALES, [P, S], U8, "vs_win"))
+        load_scale_rows(vs_win, vs_scales)
+        w2s_dealt = sb.tile([P, R], U8, name="w2s_dealt", align_bytes=ALIGN)
+        deal_scales(w2s_spread, w2s_dealt, 0, PACK)
+        w2_dealt = shared("w2_dealt", [P, R], I32, "w2_dealt")
         nc.vector.tensor_copy(
             w2_dealt[:].rearrange("p (t m) -> p t m", t=PACK), w2_raw[:].rearrange("p (m t) -> p t m", t=PACK)
         )
         pv = []
         for t in range(PACK):
-            acc = slot_product(w2_dealt[:, P * t : P * (t + 1)].bitcast(FP8X4), w2_sc[:, P * t : P * (t + 1)], 0, J)
-            b_abs = after("b_abs%d" % t, [P, J], F32, "b_abs%d" % t)
-            magnitude(b_abs[:], acc)
-            pv.append(zeroed(nc.gpsimd, after("slot%d" % t, [P, C], F32, "pv%d" % t)))
+            cols = slice(P * t, P * (t + 1))
+            acc = slot_product(w2_dealt[:, cols].bitcast(FP8X4), w2s_dealt[:, cols], 0, J)
+            b_abs = shared("b_abs%d" % t, [P, J], F32, "b_abs%d" % t)
+            b_sb = ring.tile([P, J], F32, name="b_sb")
+            nc.vector.tensor_copy(b_sb[:], acc[:])
+            nc.vector.scalar_tensor_tensor(b_abs[:], acc[:], -1.0, b_sb[:], ALU.mult, ALU.max)
+            pv.append(zeroed(nc.gpsimd, shared("a_then_pv%d" % t, [P, C], F32, "pv%d" % t)))
             scatter(pv[t], pv_list, b_abs, 0, J)
 
-        vg_sc = sb.tile([P, N], U8, name="vg_sc", align_bytes=64)
+        vg_sc = sb.tile([P, N], U8, name="vg_sc", align_bytes=ALIGN)
         nc.vector.tensor_copy(vg_sc[:], vs_win[:].indirect(vs_list[:]))
-        vg = sb.tile([P, N], U32, name="vg", align_bytes=64)
+        vg = sb.tile([P, N], U32, name="vg", align_bytes=ALIGN)
         nc.vector.tensor_copy(vg[:], vw_win[:].bitcast(U32).indirect(vs_list[:]))
 
         pages = [
-            [placed(0, [P, U], F32, "m0_0"), placed(4096, [P, U], F32, "m1_0")],
-            [after("w2_dealt", [P, U], F32, "m0_1"), after("b_abs0", [P, U], F32, "m1_1")],
+            [placed(AT_PAGES[0], [P, U], F32, "m0_0"), placed(AT_PAGES[1], [P, U], F32, "m1_0")],
+            [shared("w2_dealt", [P, U], F32, "m0_1"), shared("b_abs0", [P, U], F32, "m1_1")],
         ]
-        for g in range(N // P):
-            for side in range(2):
-                zeroed(nc.gpsimd, pages[g][side])
+        for page_pair in pages:
+            for page in page_pair:
+                zeroed(nc.gpsimd, page)
 
-        hid = [sb.tile([P, hi - lo, PACK], BF16, name="hid%d" % lo, align_bytes=64) for lo, hi in BOARD_CHUNKS]
-
-        pw_abs = after("xg", [P, PACK, C], F32, "pw_abs")
+        hid = [sb.tile([P, hi - lo, PACK], BF16, name="hid%d" % lo, align_bytes=ALIGN) for lo, hi in BOARD_CHUNKS]
+        pw_abs = shared("xg", [P, PACK, C], F32, "pw_abs")
         for t in range(PACK):
             nc.vector.scalar_tensor_tensor(pw_abs[:, t, :], pw[t][:], -1.0, pw[t][:], ALU.mult, ALU.max)
 
@@ -207,17 +220,18 @@ def tile_picked_tokens_plain_twin_bothlanded_store_divergence_kernel(
         for t in range(PACK - 1):
             for i in range(len(BOARD_CHUNKS)):
                 meet(t, i)
-        p_sb = [sb.tile([P, C], F32, name="p_sb%d" % g, align_bytes=64) for g in range(N // P)]
+        p_sb = [sb.tile([P, C], F32, name="p_sb%d" % g, align_bytes=ALIGN) for g in range(N // P)]
         for i, (lo, hi) in enumerate(BOARD_CHUNKS):
             meet(PACK - 1, i)
-            codes = sb.tile([P, hi - lo], U32, name="codes%d" % lo, align_bytes=64)
-            scales = sb.tile([P, hi - lo], U8, name="scales%d" % lo, align_bytes=64)
-            nc.vector.quantize_mx(codes[:].bitcast(FP8X4), scales[:], hid[i][:].rearrange("p c t -> p (c t)"))
+            hid_words = sb.tile([P, hi - lo], U32, name="hid_words%d" % lo, align_bytes=ALIGN)
+            hid_sc = sb.tile([P, hi - lo], U8, name="hid_sc%d" % lo, align_bytes=ALIGN)
+            nc.vector.quantize_mx(hid_words[:].bitcast(FP8X4), hid_sc[:], hid[i][:].rearrange("p c t -> p (c t)"))
             for g in range(N // P):
+                rows = slice(P * g, P * (g + 1))
                 acc = psum.tile([P, hi - lo], F32, name="acc", tag="bank")
                 nc.tensor.matmul_mx(
-                    out=acc[:], lhsT=vg[:, P * g : P * (g + 1)].bitcast(FP8X4), lhsT_scale=vg_sc[:, P * g : P * (g + 1)],
-                    rhs=codes[:].bitcast(FP8X4), rhs_scale=scales[:], start=True, stop=True,
+                    out=acc[:], lhsT=vg[:, rows].bitcast(FP8X4), lhsT_scale=vg_sc[:, rows],
+                    rhs=hid_words[:].bitcast(FP8X4), rhs_scale=hid_sc[:], start=True, stop=True,
                 )
                 if i == 0:
                     nc.scalar.copy(p_sb[g][:, lo:hi], acc[:])
@@ -225,11 +239,11 @@ def tile_picked_tokens_plain_twin_bothlanded_store_divergence_kernel(
                     nc.vector.tensor_copy(p_sb[g][:, lo:hi], acc[:])
 
         for g, lo, hi in PAGE_PIECES:
-            for side in range(2):
-                scatter(pages[g][side], page_lists[side], p_sb[g], lo, hi)
-        for g in range(N // P):
-            for lo, hi in STORE_PIECES:
-                cols = slice(lo, hi)
-                diff = sb.tile([P, hi - lo], F32, name="diff%d_%d" % (g, lo), align_bytes=64)
-                nc.vector.tensor_tensor(diff[:], pages[g][0][:, cols], pages[g][1][:, cols], ALU.subtract)
+            for page, page_list in zip(pages[g], page_lists):
+                scatter(page, page_list, p_sb[g], lo, hi)
+        for g, (m0, m1) in enumerate(pages):
+            for lo in range(0, U, STORE_COLS):
+                cols = slice(lo, lo + STORE_COLS)
+                diff = sb.tile([P, STORE_COLS], F32, name="diff%d_%d" % (g, lo), align_bytes=ALIGN)
+                nc.vector.tensor_tensor(diff[:], m0[:, cols], m1[:, cols], ALU.subtract)
                 nc.sync.dma_start(out[P * g : P * (g + 1), cols], diff[:])

@@ -19,7 +19,6 @@ ALU = mybir.AluOpType
 P = 128
 PACK = 4
 QUAD = 32
-HALF = 64
 LIST_ROWS = 16
 ALIGN = 64
 
@@ -90,15 +89,13 @@ def tile_picked_tokens_plain_twin_bothlanded_store_divergence_kernel(
 
         tok_list = load_list(offs, "tok_list")
         ws_rows = sb.tile([PACK, PACK, R // 4], I32, name="ws_rows", align_bytes=ALIGN)
-        nc.scalar.dma_start(ws_rows[:], w_scales[0].bitcast(I32).rearrange("(q i) c -> i q c", i=PACK))
-        xs_rows = sb.tile([P, 2, T // 4], I32, name="xs_rows", align_bytes=ALIGN)
-        for half, queue in enumerate((nc.sync, nc.scalar)):
-            queue.dma_start(
-                xs_rows[HALF * half : HALF * half + PACK, :, :],
-                xt_scales[0, 8 * half : 8 * half + 8, :].bitcast(I32).rearrange("(q i) c -> i q c", i=PACK),
-            )
+        nc.sync.dma_start(ws_rows[:], w_scales[0].bitcast(I32).rearrange("(q i) c -> i q c", i=PACK))
         w_raw = sb.tile([P, 2 * R], U8, name="w_raw", align_bytes=ALIGN)
         nc.sync.dma_start(w_raw[:].bitcast(I32), w_words[0].bitcast(I32))
+        xs_win = sb.tile([P, T], U8, name="xs_win", align_bytes=ALIGN)
+        nc.vector.memset(xs_win[:, : T // 2].bitcast(I32), 0)
+        nc.gpsimd.memset(xs_win[:, T // 2 :].bitcast(I32), 0)
+        load_scale_rows(xs_win, xt_scales)
         xw_win = placed(AT_TOKEN_WORDS, [P, T], I32, "xw_win")
         nc.sync.dma_start(xw_win[:], words_view(xt_words))
         pw_list = load_list(offs2, "pw_list")
@@ -107,7 +104,6 @@ def tile_picked_tokens_plain_twin_bothlanded_store_divergence_kernel(
         page_lists = [load_list(offs5, "m0_list"), load_list(offs6, "m1_list")]
 
         ws_spread = zeroed(nc.vector, sb.tile([P, R], U8, name="ws_spread", align_bytes=ALIGN))
-        xs_win = zeroed(nc.vector, sb.tile([P, T], U8, name="xs_win", align_bytes=ALIGN))
         pw = [
             zeroed(nc.vector, sb.tile([P, C], F32, name="pw%d" % t, align_bytes=ALIGN)) for t in range(EARLY_BOARDS)
         ]
@@ -120,11 +116,6 @@ def tile_picked_tokens_plain_twin_bothlanded_store_divergence_kernel(
             w_dealt[:].bitcast(U16).rearrange("p (t m) -> p t m", t=PACK),
             w_raw[:].bitcast(U16).rearrange("p (m t) -> p t m", t=PACK),
         )
-        for q in range(PACK):
-            row0 = HALF * (q // 2)
-            nc.vector.tensor_copy(
-                xs_win[QUAD * q : QUAD * q + PACK, :].bitcast(I32), xs_rows[row0 : row0 + PACK, q % 2, :]
-            )
         xg_sc_early = sb.tile([P, SCALE_GATHER], U8, name="xg_sc_early", align_bytes=ALIGN)
         nc.vector.tensor_copy(xg_sc_early[:], xs_win[:].indirect(entries(tok_list, 0, SCALE_GATHER)))
         xg = shared("xg", [P, J], U32, "xg")

from contextlib import ExitStack

import concourse.mybir as mybir

K, J, R, T, C, N, S, U = 512, 384, 512, 2048, 512, 256, 1024, 1024
FLOPS = 2 * (2 * K * R * J + R * N * C)

F32 = mybir.dt.float32
BF16 = mybir.dt.bfloat16
I32 = mybir.dt.int32
U32 = mybir.dt.uint32
U16 = mybir.dt.uint16
U8 = mybir.dt.uint8
FP8X4 = mybir.dt.float8_e4m3fn_x4
FP4X4 = mybir.dt.float4_e2m1fn_x4
ACT = mybir.ActivationFunctionType
ALU = mybir.AluOpType

P = 128
PACK = 4
QUAD = 32
LIST_ROWS = 16
ALIGN = 64

WORD_GATHER = 128
SCALE_GATHER = 256
EARLY_BOARDS = 2
FIRST_BOARD_PIECES = ((0, 0, 128), (1, 0, 256), (0, 128, J), (1, 256, J), (2, 0, J), (3, 0, J))
BOARD_CHUNKS = ((0, 64), (64, 128), (128, 256), (256, 384), (384, 512))
PAGE_PIECES = ((0, 0, 64), (1, 0, 64), (0, 64, 256), (0, 256, C), (1, 64, C))
STORE_COLS = 256

AT_TOKEN_WORDS = 0
AT_STORE_WORDS = 0
AT_W2_WORDS = 4096
AT_W_SCALES_LATE = 6528
AT_SLOT_SCALES_LATE = 7936
AT_W2_SCALES = 6144
AT_STORE_SCALES = 6656
AT_PAGES = (0, 4096)


def tile_picked_tokens_plain_twin_bothlanded_store_divergence_kernel(
    tc, xt_words, xt_scales, w_words, w_scales, w2_words, w2_scales, vs_words, vs_scales,
    offs, offs2, offs3, offs4, offs5, offs6, out,
):
    nc = tc.nc

    with ExitStack() as ctx:
        lists = ctx.enter_context(tc.tile_pool(name="lists", bufs=1))
        sb = ctx.enter_context(tc.tile_pool(name="sb", bufs=1))
        reuse = ctx.enter_context(tc.tile_pool(name="reuse", bufs=1))
        ring = ctx.enter_context(tc.tile_pool(name="ring", bufs=2))
        psum = ctx.enter_context(tc.psum_pool(name="psum", bufs=8))

        def load_list(dram, name):
            tile = lists.tile(list(dram.shape), U16, name=name)
            nc.sync.dma_start(tile[:], dram)
            return tile

        def entries(list_tile, lo, hi):
            return list_tile[:, lo // LIST_ROWS : hi // LIST_ROWS]

        def words_view(dram):
            return dram[0].rearrange("p c b -> p (c b)").bitcast(I32)

        def zeroed(engine, tile):
            engine.memset(tile[:].bitcast(I32), 0)
            return tile

        def shared(tag, shape, dtype, name):
            return sb.tile(shape, dtype, name=name, tag=tag, align_bytes=ALIGN)

        def placed(offset, shape, dtype, name):
            return reuse.tile(shape, dtype, name=name, offset=offset, align_bytes=ALIGN)

        def load_scale_rows(tile, dram):
            for q in range(PACK):
                nc.sync.dma_start(
                    tile[QUAD * q : QUAD * q + PACK, :].bitcast(I32),
                    dram[0, PACK * q : PACK * (q + 1), :].bitcast(I32),
                )

        def deal_scales(scales, dealt, t0, t1):
            nc.vector.tensor_copy(
                dealt[:].rearrange("p (t m) -> p t m", m=P),
                scales[:].rearrange("p (m t) -> p t m", t=PACK)[:, t0:t1, :],
            )

        tok_list = load_list(offs, "tok_list")
        ws_rows = sb.tile([PACK, PACK, R // 4], I32, name="ws_rows", align_bytes=ALIGN)
        nc.sync.dma_start(ws_rows[:], w_scales[0].bitcast(I32).rearrange("(q i) c -> i q c", i=PACK))
        w_raw = sb.tile([P, 2 * R], U8, name="w_raw", align_bytes=ALIGN)
        nc.sync.dma_start(w_raw[:].bitcast(I32), w_words[0].bitcast(I32))
        xs_win = sb.tile([P, T], U8, name="xs_win", align_bytes=ALIGN)
        nc.vector.memset(xs_win[:, : T // 2].bitcast(I32), 0)
        nc.gpsimd.memset(xs_win[:, T // 2 :].bitcast(I32), 0)
        load_scale_rows(xs_win, xt_scales)
        xw_win = placed(AT_TOKEN_WORDS, [P, T], I32, "xw_win")
        nc.sync.dma_start(xw_win[:], words_view(xt_words))
        pw_list = load_list(offs2, "pw_list")
        pv_list = load_list(offs3, "pv_list")
        vs_list = load_list(offs4, "vs_list")
        page_lists = [load_list(offs5, "m0_list"), load_list(offs6, "m1_list")]

        ws_spread = zeroed(nc.vector, sb.tile([P, R], U8, name="ws_spread", align_bytes=ALIGN))
        pw = [
            zeroed(nc.vector, sb.tile([P, C], F32, name="pw%d" % t, align_bytes=ALIGN)) for t in range(EARLY_BOARDS)
        ]
        for q in range(PACK):
            nc.vector.tensor_copy(ws_spread[QUAD * q : QUAD * q + PACK, :].bitcast(I32), ws_rows[:, q, :])
        ws_dealt = [shared("ws_early", [P, EARLY_BOARDS * P], U8, "ws_early")]
        deal_scales(ws_spread, ws_dealt[0], 0, EARLY_BOARDS)
        w_dealt = shared("w_dealt", [P, 2 * R], U8, "w_dealt")
        nc.scalar.copy(
            w_dealt[:].bitcast(U16).rearrange("p (t m) -> p t m", t=PACK),
            w_raw[:].bitcast(U16).rearrange("p (m t) -> p t m", t=PACK),
        )
        xg_sc_early = sb.tile([P, SCALE_GATHER], U8, name="xg_sc_early", align_bytes=ALIGN)
        nc.vector.tensor_copy(xg_sc_early[:], xs_win[:].indirect(entries(tok_list, 0, SCALE_GATHER)))
        xg = shared("xg", [P, J], U32, "xg")
        for lo in range(0, J, WORD_GATHER):
            hi = lo + WORD_GATHER
            nc.vector.tensor_copy(xg[:, lo:hi], xw_win[:].bitcast(U32).indirect(entries(tok_list, lo, hi)))
        xg_sc_late = placed(AT_SLOT_SCALES_LATE, [P, SCALE_GATHER], U8, "xg_sc_late")
        nc.vector.tensor_copy(xg_sc_late[:], xs_win[:].indirect(entries(tok_list, J - SCALE_GATHER, J)))
        ws_dealt.append(placed(AT_W_SCALES_LATE, [P, (PACK - EARLY_BOARDS) * P], U8, "ws_late"))
        deal_scales(ws_spread, ws_dealt[1], EARLY_BOARDS, PACK)

        def slot_product(weights, weight_scales, lo, hi):
            acc = psum.tile([P, hi - lo], F32, name="acc", tag="bank")
            for base, slot_scales, c0, c1 in (
                (0, xg_sc_early, lo, min(hi, SCALE_GATHER)),
                (J - SCALE_GATHER, xg_sc_late, max(lo, SCALE_GATHER), hi),
            ):
                if c0 < c1:
                    nc.tensor.matmul_mx(
                        out=acc[:, c0 - lo : c1 - lo], lhsT=weights, lhsT_scale=weight_scales,
                        rhs=xg[:, c0:c1].bitcast(FP8X4), rhs_scale=slot_scales[:, c0 - base : c1 - base],
                        start=True, stop=True,
                    )
            return acc

        def scatter(window, list_tile, values, lo, hi):
            nc.scalar.activation(window[:].indirect(entries(list_tile, lo, hi)), values[:, lo:hi], ACT.Copy)

        a_sb = [shared("a_then_pv%d" % t, [P, J], F32, "a_sb%d" % t) for t in range(PACK)]
        for i, (t, lo, hi) in enumerate(FIRST_BOARD_PIECES):
            part, place = divmod(t, EARLY_BOARDS)
            acc = slot_product(
                w_dealt[:, 2 * P * t : 2 * P * (t + 1)].bitcast(FP4X4),
                ws_dealt[part][:, P * place : P * (place + 1)], lo, hi,
            )
            if i == 0:
                nc.scalar.activation(a_sb[t][:, lo:hi], acc[:], ACT.Copy)
            else:
                nc.vector.tensor_copy(a_sb[t][:, lo:hi], acc[:])
            if t < EARLY_BOARDS:
                scatter(pw[t], pw_list, a_sb[t], lo, hi)
        for t, tag in zip(range(EARLY_BOARDS, PACK), ("w_dealt", "ws_early")):
            pw.append(zeroed(nc.gpsimd, shared(tag, [P, C], F32, "pw%d" % t)))
            scatter(pw[t], pw_list, a_sb[t], 0, J)

        w2_raw = placed(AT_W2_WORDS, [P, R], I32, "w2_raw")
        nc.sync.dma_start(w2_raw[:], words_view(w2_words))
        w2s_spread = zeroed(nc.gpsimd, placed(AT_W2_SCALES, [P, R], U8, "w2s_spread"))
        load_scale_rows(w2s_spread, w2_scales)
        vw_win = placed(AT_STORE_WORDS, [P, S], I32, "vw_win")
        nc.sync.dma_start(vw_win[:], words_view(vs_words))
        vs_win = zeroed(nc.gpsimd, placed(AT_STORE_SCALES, [P, S], U8, "vs_win"))
        load_scale_rows(vs_win, vs_scales)
        w2s_dealt = sb.tile([P, R], U8, name="w2s_dealt", align_bytes=ALIGN)
        deal_scales(w2s_spread, w2s_dealt, 0, PACK)
        w2_dealt = shared("w2_dealt", [P, R], I32, "w2_dealt")
        nc.vector.tensor_copy(
            w2_dealt[:].rearrange("p (t m) -> p t m", t=PACK), w2_raw[:].rearrange("p (m t) -> p t m", t=PACK)
        )
        pv = []
        for t in range(PACK):
            cols = slice(P * t, P * (t + 1))
            acc = slot_product(w2_dealt[:, cols].bitcast(FP8X4), w2s_dealt[:, cols], 0, J)
            b_abs = shared("b_abs%d" % t, [P, J], F32, "b_abs%d" % t)
            b_sb = ring.tile([P, J], F32, name="b_sb")
            nc.vector.tensor_copy(b_sb[:], acc[:])
            nc.vector.scalar_tensor_tensor(b_abs[:], acc[:], -1.0, b_sb[:], ALU.mult, ALU.max)
            pv.append(zeroed(nc.gpsimd, shared("a_then_pv%d" % t, [P, C], F32, "pv%d" % t)))
            scatter(pv[t], pv_list, b_abs, 0, J)

        vg_sc = sb.tile([P, N], U8, name="vg_sc", align_bytes=ALIGN)
        nc.vector.tensor_copy(vg_sc[:], vs_win[:].indirect(vs_list[:]))
        vg = sb.tile([P, N], U32, name="vg", align_bytes=ALIGN)
        nc.vector.tensor_copy(vg[:], vw_win[:].bitcast(U32).indirect(vs_list[:]))

        pages = [
            [placed(AT_PAGES[0], [P, U], F32, "m0_0"), placed(AT_PAGES[1], [P, U], F32, "m1_0")],
            [shared("w2_dealt", [P, U], F32, "m0_1"), shared("b_abs0", [P, U], F32, "m1_1")],
        ]
        for page_pair in pages:
            for page in page_pair:
                zeroed(nc.gpsimd, page)

        hid = [sb.tile([P, hi - lo, PACK], BF16, name="hid%d" % lo, align_bytes=ALIGN) for lo, hi in BOARD_CHUNKS]
        pw_abs = shared("xg", [P, PACK, C], F32, "pw_abs")
        for t in range(PACK):
            nc.vector.scalar_tensor_tensor(pw_abs[:, t, :], pw[t][:], -1.0, pw[t][:], ALU.mult, ALU.max)

        def meet(t, i):
            lo, hi = BOARD_CHUNKS[i]
            nc.vector.tensor_tensor(hid[i][:, :, t], pw_abs[:, t, lo:hi], pv[t][:, lo:hi], ALU.min)

        for t in range(PACK - 1):
            for i in range(len(BOARD_CHUNKS)):
                meet(t, i)
        p_sb = [sb.tile([P, C], F32, name="p_sb%d" % g, align_bytes=ALIGN) for g in range(N // P)]
        for i, (lo, hi) in enumerate(BOARD_CHUNKS):
            meet(PACK - 1, i)
            hid_words = sb.tile([P, hi - lo], U32, name="hid_words%d" % lo, align_bytes=ALIGN)
            hid_sc = sb.tile([P, hi - lo], U8, name="hid_sc%d" % lo, align_bytes=ALIGN)
            nc.vector.quantize_mx(hid_words[:].bitcast(FP8X4), hid_sc[:], hid[i][:].rearrange("p c t -> p (c t)"))
            for g in range(N // P):
                rows = slice(P * g, P * (g + 1))
                acc = psum.tile([P, hi - lo], F32, name="acc", tag="bank")
                nc.tensor.matmul_mx(
                    out=acc[:], lhsT=vg[:, rows].bitcast(FP8X4), lhsT_scale=vg_sc[:, rows],
                    rhs=hid_words[:].bitcast(FP8X4), rhs_scale=hid_sc[:], start=True, stop=True,
                )
                if i == 0:
                    nc.scalar.copy(p_sb[g][:, lo:hi], acc[:])
                else:
                    nc.vector.tensor_copy(p_sb[g][:, lo:hi], acc[:])

        for g, lo, hi in PAGE_PIECES:
            for page, page_list in zip(pages[g], page_lists):
                scatter(page, page_list, p_sb[g], lo, hi)
        for g, (m0, m1) in enumerate(pages):
            for lo in range(0, U, STORE_COLS):
                cols = slice(lo, lo + STORE_COLS)
                diff = sb.tile([P, STORE_COLS], F32, name="diff%d_%d" % (g, lo), align_bytes=ALIGN)
                nc.vector.tensor_tensor(diff[:], m0[:, cols], m1[:, cols], ALU.subtract)
                nc.sync.dma_start(out[P * g : P * (g + 1), cols], diff[:])
